import numpy as np
import ml_dtypes


def mxq(x, axis, fmt="e4m3"):
    dtype, down = {"e4m3": (ml_dtypes.float8_e4m3fn, 7), "e5m2": (ml_dtypes.float8_e5m2, 14)}[fmt]
    v = np.moveaxis(np.asarray(x, np.float32).astype(ml_dtypes.bfloat16).astype(np.float64), axis, -1)
    blocks = v.reshape(v.shape[:-1] + (-1, 32))
    amax = np.abs(blocks).max(-1, keepdims=True)
    byte = np.maximum(np.where(amax > 0, np.frexp(amax)[1] - 1 + 127, 0) - down, 1)
    scale = np.exp2(byte - 127.0)
    codes = (blocks / scale).astype(np.float32).astype(dtype).astype(np.float64)
    return np.moveaxis((codes * scale).reshape(v.shape), -1, axis)


WIDE = False


def mx_kscale(k, group=512):
    if not WIDE:
        return np.ones(k)
    levels = np.array([10, -10, 5, -5, 0])
    if group != 512:
        return np.exp2(np.random.permutation(np.resize(levels, k // group))).repeat(group)
    if k % 512:
        return np.exp2(np.random.permutation(np.resize(levels, k // 32))).repeat(32)
    a = np.empty((k // 512, 16))
    for p in range(k // 512):
        a[p, :8] = np.random.permutation(np.resize(levels, 8))
        for g in range(8):
            far = levels[np.abs(levels - a[p, g]) >= 10]
            a[p, g + 8] = far[np.random.randint(len(far))]
    return np.exp2(a.ravel()).repeat(32)


def f64(x):
    return np.asarray(x).astype(np.float64)


def striped(idx):
    return np.tile(np.asarray(idx).reshape(-1, 16).T, (8, 1)).astype(np.uint16)


def unstriped(offs):
    return offs[:16].T.reshape(-1).astype(np.int64)


H, KV, D, NQ, N = 4, 2, 256, 512, 512


def setup_inputs():
    n = np.random.standard_normal
    s = mx_kscale(D, 0)[:, None]
    u = mx_kscale(N)
    t = np.random.uniform(0.5, 2.0, N) * u
    v = n((KV, N, 128))
    return {
        "qT": (n((H, D, NQ)) * s * (0.70 / np.sqrt(D))).astype(np.float32),
        "kT": (n((KV, D, N)) / s).astype(np.float32),
        "t": t.reshape(N, 1).astype(np.float32),
        "v": (v / t[:, None]).astype(np.float32),
        "kb": (0.5 * n((N, 1))).astype(np.float32),
        "mask": (np.arange(N)[:, None] <= np.sort(np.random.randint(N // 4, N, NQ))[None, :]).astype(np.float32),
    }


def reference(qT, kT, t, v, kb, mask):
    a = np.repeat(mxq(f64(kT), 1, "e4m3"), H // KV, 0).transpose(0, 2, 1) @ mxq(f64(qT), 1, "e4m3")
    a = a + f64(kb)
    p = a / (1.0 + np.exp(-a))
    p = p * f64(mask)
    w = p * f64(t)
    y = mxq(w, 1, "e4m3").transpose(0, 2, 1) @ np.repeat(mxq(f64(v), 1, "e4m3"), H // KV, 0)
    y = y / 16.0
    return y

@@ -1,0 +1,250 @@
+from contextlib import ExitStack
+
+import concourse.mybir as mybir
+
+RANGES = [128, 256, 128]
+JOINT = [0, 0, 0]
+RUN = 2
+ORDER = """
+Lk:Y LqA0:Y dA0:S Lm0:Y LqB0:Y dB0:S ck0:V ck1:S cqA0:V Qk0:V LqA1:Y dA1:S
+Lm1:Y Lv:Y QqA0:V Qk1:V mt00:S sA00:P mt01:V sA01:P aA010:S cqB0:V aA011:S QqB0:V
+aA000:S TA01:V aA001:S sB01:P sB00:P cqA1:V aB001:S aB011:S TA00:V LqB1:Y dB1:S aB000:S
+QqA1:V aB010:S WA00:V TB00:V mt10:S sA10:P TB01:V LqA2:Y dA2:S Lm2:Y sA11:P mt11:S
+cv0:V aA100:S cv1:V WA01:V WB00:V aA101:S Qv:V cqB1:V LqB2:Y dB2:S pB00:P aA110:S
+pA00:P WB01:V eB00:V eA00:S QqB1:V pB01:P cqA2:S pA01:P TA10:V sB10:P aA111:S sB11:P
+eB01:S QqA2:V eA01:S cqB2:V aB100:S WA10:V QqB2:V TA11:V aB101:S sB21:P pA10:P aB110:S
+TB10:V aB111:S sB20:P aB201:S sA21:P WA11:V aB211:S WB10:V mt21:S sA20:P TB11:V aB200:S
+pB10:P mt20:S aB210:S TB20:V eA10:S aA211:S pA11:P WB11:V aA210:S WB20:V TB21:V aA200:S
+eB10:S TA21:V aA201:S pB11:P eA11:S WB21:V TA20:V eB11:S pB20:P pB21:P WA21:V eB20:S
+WA20:V eB21:S pA21:P pA20:P eA21:V eA20:V
+"""
+
+F32 = mybir.dt.float32
+BF16 = mybir.dt.bfloat16
+U32 = mybir.dt.uint32
+U8 = mybir.dt.uint8
+FP8X4 = mybir.dt.float8_e4m3fn_x4
+ACT = mybir.ActivationFunctionType
+ALU = mybir.AluOpType
+
+H, KV, D, NQ, N, E = 4, 2, 256, 512, 512, 128
+P = 128
+ROWS = 64
+PACK = 4
+FLOPS = 2 * H * NQ * N * (D + E)
+
+
+def tile_rows_a_silu_kb_mask_kernel(tc, qT, kT, t, v, kb, mask, out):
+    nc = tc.nc
+    starts = [sum(RANGES[:i]) for i in range(len(RANGES))]
+    with ExitStack() as ctx:
+        sb = ctx.enter_context(tc.tile_pool(name="sb", bufs=1))
+        ps = ctx.enter_context(tc.psum_pool(name="ps", bufs=1))
+        ctx.enter_context(tc.manual_schedule())
+
+        def tile(name, shape, dtype):
+            return sb.tile(shape, dtype, name=name, align_bytes=64)
+
+        score_banks = [[ps.tile([P, 512], F32, name="score%d%d" % (g, b)) for b in range(3)] for g in range(2)]
+        y_banks = [ps.tile([P, 512], F32, name="ybank%d" % b) for b in range(2)]
+        used = {"s": 0, "y": 0}
+        where = {}
+
+        t_sb = tile("t_sb", [P, PACK], F32)
+        kb_sb = tile("kb_sb", [P, PACK], F32)
+        warm = tile("warm", [P, 2], F32)
+        k_raw = tile("k_raw", [P, PACK, N], F32)
+        k_bf = [tile("k_bf%d" % x, [P, 2, P, PACK], BF16) for x in range(2)]
+        k_codes = [tile("k_codes%d" % x, [P, 2 * P], U32) for x in range(2)]
+        k_scales = [tile("k_scales%d" % x, [P, 2 * P], U8) for x in range(2)]
+        v_raw = tile("v_raw", [P, KV, PACK, E], F32)
+        v_bf = tile("v_bf", [P, KV, E, PACK], BF16)
+        v_codes = tile("v_codes", [P, KV * E], U32)
+        v_scales = tile("v_scales", [P, KV * E], U8)
+        m_raw, mt, q_raw, q_bf, q_codes, q_scales = {}, {}, {}, {}, {}, {}
+        p_sb, w_bf, w_codes, w_scales, y_sb = {}, {}, {}, {}, {}
+        for i, W in enumerate(RANGES):
+            m_raw[i] = tile("m_raw%d" % i, [P, PACK, W], F32)
+            mt[i] = tile("mt%d" % i, [P, PACK, W], F32)
+            for s in ["AB"] if JOINT[i] else "AB":
+                for g in range(2):
+                    both = tile("p_sb%s%d%d" % (s, i, g), [P, PACK, len(s), W], F32)
+                    p_sb[s, i, g] = both[:].rearrange("p r s n -> p r (s n)")
+                    for x, c in enumerate(s):
+                        p_sb[c + str(i) + str(g)] = both[:, :, x, :]
+            for s in "AB":
+                u = s + str(i)
+                q_raw[u] = tile("q_raw" + u, [P, PACK, W], F32)
+                q_bf[u] = tile("q_bf" + u, [P, W, PACK], BF16)
+                q_codes[u] = tile("q_codes" + u, [P, W], U32)
+                q_scales[u] = tile("q_scales" + u, [P, W], U8)
+                for g in range(2):
+                    n = u + str(g)
+                    w_bf[n] = tile("w_bf" + n, [P, W, PACK], BF16)
+                    w_codes[n] = tile("w_codes" + n, [P, W], U32)
+                    w_scales[n] = tile("w_scales" + n, [P, W], U8)
+                    y_sb[n] = tile("y_sb" + n, [P, W], F32)
+
+        def copy(eng, dst, src):
+            if eng == "V":
+                nc.vector.tensor_copy(out=dst, in_=src)
+            else:
+                nc.scalar.copy(out=dst, in_=src)
+
+        def quantize(codes, scales, src):
+            nc.vector.quantize_mx(out=codes[:].bitcast(FP8X4), scales=scales[:], in_=src)
+
+        def load_q(queue, u, g):
+            i = int(u[1])
+            h = 2 * g + "AB".index(u[0])
+            cols = slice(starts[i], starts[i] + RANGES[i])
+            queue.dma_start(
+                out=q_raw[u][ROWS * g : ROWS * (g + 1), :, :],
+                in_=qT[h].rearrange("(p j) n -> p j n", j=PACK)[:, :, cols],
+            )
+
+        def load(name):
+            if name == "k":
+                nc.sync.dma_start(out=k_raw[:], in_=kT.rearrange("g (p j) n -> (g p) j n", j=PACK))
+            elif name == "v":
+                nc.sync.dma_start(
+                    out=v_raw[:].rearrange("p g j e -> p g (j e)"),
+                    in_=v.rearrange("g (p j) e -> p g (j e)", j=PACK),
+                )
+            elif name[0] == "m":
+                i = int(name[1])
+                cols = slice(starts[i], starts[i] + RANGES[i])
+                nc.sync.dma_start(out=m_raw[i][:], in_=mask.rearrange("(p j) n -> p j n", j=PACK)[:, :, cols])
+            else:
+                load_q(nc.sync, name[1:], 0)
+
+        nc.scalar.dma_start(out=kb_sb[:], in_=kb.rearrange("(p j) o -> p (j o)", j=PACK))
+        nc.scalar.dma_start(out=t_sb[:], in_=t.rearrange("(p j) o -> p (j o)", j=PACK))
+        nc.vector.memset(warm[:, 0:1], 0.0)
+        nc.scalar.activation(out=warm[:, 1:2], in_=warm[:, 0:1], func=ACT.Silu)
+
+        for step in ORDER.split():
+            name, eng = step.split(":")
+            kind = name[0]
+            if kind == "L":
+                load(name[1:])
+            elif kind == "d":
+                load_q(nc.scalar, name[1:], 1)
+            elif name[:2] == "ck":
+                x = int(name[2])
+                copy(
+                    eng,
+                    k_bf[x][:].rearrange("p r s j -> p s j r"),
+                    k_raw[:].rearrange("p j (s r) -> p s j r", r=PACK)[:, :, :, 2 * x : 2 * x + 2],
+                )
+            elif name[:2] == "Qk":
+                x = int(name[2])
+                quantize(k_codes[x], k_scales[x], k_bf[x][:].rearrange("p r s j -> p (r s j)"))
+            elif name[:2] == "cv":
+                g = int(name[2])
+                copy(
+                    eng,
+                    v_bf[:, g].rearrange("p (c i) j -> p c j i", i=RUN),
+                    v_raw[:, g].rearrange("p j (c i) -> p c j i", i=RUN),
+                )
+            elif name == "Qv":
+                quantize(v_codes, v_scales, v_bf[:].rearrange("p g e j -> p (g e j)"))
+            elif name[:2] == "mt":
+                i = int(name[2])
+                for r in (2 * int(name[3]), 2 * int(name[3]) + 1):
+                    if eng == "V":
+                        nc.vector.tensor_scalar(
+                            out=mt[i][:, r, :], in0=m_raw[i][:, r, :], scalar1=t_sb[:, r : r + 1], scalar2=None, op0=ALU.mult
+                        )
+                    else:
+                        nc.scalar.activation(out=mt[i][:, r, :], in_=m_raw[i][:, r, :], func=ACT.Copy, scale=t_sb[:, r : r + 1])
+            elif name[:2] == "cq":
+                u = name[2:]
+                copy(
+                    eng,
+                    q_bf[u][:].rearrange("p (c i) j -> p c j i", i=RUN),
+                    q_raw[u][:].rearrange("p j (c i) -> p c j i", i=RUN),
+                )
+            elif name[:2] == "Qq":
+                u = name[2:]
+                quantize(q_codes[u], q_scales[u], q_bf[u][:].rearrange("p n j -> p (n j)"))
+            elif kind == "s":
+                i, b = int(name[2]), int(name[3])
+                sets = "AB" if name[1] == "J" else name[1]
+                W = RANGES[i]
+                per = 2 if W * len(sets) <= 256 else 1
+                slot = used["s"] % 3
+                used["s"] += 1
+                where[name] = slot
+                col = 0
+                for r in range(per * b, per * (b + 1)):
+                    kc = slice((r % 2) * P, (r % 2 + 1) * P)
+                    for s in sets:
+                        u = s + str(i)
+                        for c in range(0, W, P):
+                            for g in range(2):
+                                rows = slice(ROWS * g, ROWS * (g + 1))
+                                nc.tensor.matmul_mx(
+                                    out=score_banks[g][slot][:, col : col + P],
+                                    lhsT=k_codes[r // 2][rows, kc].bitcast(FP8X4),
+                                    lhsT_scale=k_scales[r // 2][rows, kc],
+                                    rhs=q_codes[u][rows, c : c + P].bitcast(FP8X4),
+                                    rhs_scale=q_scales[u][rows, c : c + P],
+                                    start=True,
+                                    stop=True,
+                                )
+                            col += P
+            elif kind == "a":
+                i, g, b = int(name[2]), int(name[3]), int(name[4])
+                sets = "AB" if name[1] == "J" else name[1]
+                AW = RANGES[i] * len(sets)
+                per = 2 if AW <= 256 else 1
+                bank = score_banks[g][where["s" + name[1:3] + name[4]]]
+                for x in range(per):
+                    r = per * b + x
+                    nc.scalar.activation(
+                        out=p_sb[sets, i, g][:, r, :],
+                        in_=bank[:, x * AW : (x + 1) * AW],
+                        func=ACT.Silu,
+                        bias=kb_sb[:, r : r + 1],
+                    )
+            elif kind == "T":
+                n = name[1:]
+                nc.vector.tensor_tensor(
+                    out=w_bf[n][:].rearrange("p (c i) r -> p c r i", i=RUN),
+                    in0=p_sb[n].rearrange("p r (c i) -> p c r i", i=RUN),
+                    in1=mt[int(n[1])][:].rearrange("p r (c i) -> p c r i", i=RUN),
+                    op=ALU.mult,
+                )
+            elif kind == "W":
+                n = name[1:]
+                quantize(w_codes[n], w_scales[n], w_bf[n][:].rearrange("p n r -> p (n r)"))
+            elif kind == "p":
+                n = name[1:]
+                g = int(n[2])
+                W = RANGES[int(n[1])]
+                bank = y_banks[used["y"] % 2]
+                used["y"] += 1
+                where[n] = bank[:, 0:W]
+                for c in range(0, W, P):
+                    nc.tensor.matmul_mx(
+                        out=bank[:, c : c + P],
+                        lhsT=w_codes[n][:, c : c + P].bitcast(FP8X4),
+                        lhsT_scale=w_scales[n][:, c : c + P],
+                        rhs=v_codes[:, g * E : (g + 1) * E].bitcast(FP8X4),
+                        rhs_scale=v_scales[:, g * E : (g + 1) * E],
+                        start=True,
+                        stop=True,
+                    )
+            else:
+                n = name[1:]
+                i, g = int(n[1]), int(n[2])
+                h = 2 * g + "AB".index(n[0])
+                if eng == "V":
+                    nc.vector.tensor_scalar(out=y_sb[n][:], in0=where[n], scalar1=1.0 / 16.0, scalar2=None, op0=ALU.mult)
+                else:
+                    nc.scalar.activation(out=y_sb[n][:], in_=where[n], func=ACT.Copy, scale=1.0 / 16.0)
+                nc.sync.dma_start(
+                    out=out[h, starts[i] : starts[i] + RANGES[i], :].rearrange("(c p) e -> p c e", p=P),
+                    in_=y_sb[n][:].rearrange("p (c e) -> p c e", e=E),
+                )

@@ -2,21 +2,25 @@ from contextlib import ExitStack
 
 import concourse.mybir as mybir
 
-RANGES = [128, 256, 128]
-JOINT = [0, 0, 0]
+LOADS = {'M0': (0, 128), 'm0': (0, 128), 'O0': (0, 128), 'M1': (128, 256), 'm1': (128, 256), 'O1': (128, 256), 'M2': (384, 128), 'm2': (384, 128), 'O2': (384, 128)}
+PIECES = {'M': [(0, 128), (128, 256), (384, 128)], 'O': [(0, 128), (128, 256), (384, 128)]}
+UNITS = {'M': [(0, 128), (128, 256), (384, 128)], 'O': [(0, 128), (128, 256), (384, 128)]}
+CHUNKS = {'M': [(0, 128), (128, 256), (384, 128)], 'O': [(0, 128), (128, 256), (384, 128)]}
 RUN = 2
+PER = 128
+RING = 0
 ORDER = """
-Lk:Y LqA0:Y dA0:S Lm0:Y LqB0:Y dB0:S ck0:V ck1:S cqA0:V Qk0:V LqA1:Y dA1:S
-Lm1:Y Lv:Y QqA0:V Qk1:V mt00:S sA00:P mt01:V sA01:P aA010:S cqB0:V aA011:S QqB0:V
-aA000:S TA01:V aA001:S sB01:P sB00:P cqA1:V aB001:S aB011:S TA00:V LqB1:Y dB1:S aB000:S
-QqA1:V aB010:S WA00:V TB00:V mt10:S sA10:P TB01:V LqA2:Y dA2:S Lm2:Y sA11:P mt11:S
-cv0:V aA100:S cv1:V WA01:V WB00:V aA101:S Qv:V cqB1:V LqB2:Y dB2:S pB00:P aA110:S
-pA00:P WB01:V eB00:V eA00:S QqB1:V pB01:P cqA2:S pA01:P TA10:V sB10:P aA111:S sB11:P
-eB01:S QqA2:V eA01:S cqB2:V aB100:S WA10:V QqB2:V TA11:V aB101:S sB21:P pA10:P aB110:S
-TB10:V aB111:S sB20:P aB201:S sA21:P WA11:V aB211:S WB10:V mt21:S sA20:P TB11:V aB200:S
-pB10:P mt20:S aB210:S TB20:V eA10:S aA211:S pA11:P WB11:V aA210:S WB20:V TB21:V aA200:S
-eB10:S TA21:V aA201:S pB11:P eA11:S WB21:V TA20:V eB11:S pB20:P pB21:P WA21:V eB20:S
-WA20:V eB21:S pA21:P pA20:P eA21:V eA20:V
+Lk:Y LM0:Y Lm0:Y LO0:Y LM1:Y Lm1:Y LO1:Y LM2:Y Lm2:Y Lv:Y LO2:Y ck0:V
+ck1:S cqM0:V Qk0:V QqM0:V Qk1:V mt01:S sM00:P mt00:V sM01:P aM000:S cqO0:V aM001:S
+QqO0:V aM011:S TM00:V aM010:S sO00:P cqM1:V sO01:P aO010:S WM00:V aO000:S QqM1:V aO011:S
+TM01:V aO001:S sM11:P TO01:V mt10:S sM12:P WM01:V aM111:S TO00:V sM13:P aM101:S mt11:V
+aM102:S sM10:P aM113:S WO00:V WO01:V aM103:S cqO1:V aM112:S aM110:S cqM2:S QqO1:V TM11:V
+aM100:S sO12:P mt20:S sO10:P mt21:S TM10:V aO112:S sO13:P aO102:S cv1:S sO11:P cv0:V
+WM10:V aO100:S Qv:V aO110:S QqM2:V aO111:S cqO2:V pO01:P aO113:S pM01:P WM11:V sM20:P
+aO103:S QqO2:V eO01:S TO11:V eM01:S pM00:P aO101:S pO00:P sO20:P aM200:S eM00:S TO10:V
+sM21:P aM210:S aO200:S pM10:P sO21:P eO00:S aM211:S WO11:V WO10:V pM11:P aM201:S TM21:V
+eM10:S eM11:S pO10:P TM20:V aO201:S pO11:P aO210:S WM21:V TO20:V aO211:S eO10:S WM20:V
+TO21:V eO11:S pM20:P pM21:P WO20:V eM20:S WO21:V eM21:S pO20:P pO21:P eO20:S eO21:V
 """
 
 F32 = mybir.dt.float32
@@ -31,12 +35,12 @@ H, KV, D, NQ, N, E = 4, 2, 256, 512, 512, 128
 P = 128
 ROWS = 64
 PACK = 4
+HEADS = {"M": (1, 2), "O": (0, 3)}
 FLOPS = 2 * H * NQ * N * (D + E)
 
 
 def tile_rows_a_silu_kb_mask_kernel(tc, qT, kT, t, v, kb, mask, out):
     nc = tc.nc
-    starts = [sum(RANGES[:i]) for i in range(len(RANGES))]
     with ExitStack() as ctx:
         sb = ctx.enter_context(tc.tile_pool(name="sb", bufs=1))
         ps = ctx.enter_context(tc.psum_pool(name="ps", bufs=1))
@@ -61,29 +65,33 @@ def tile_rows_a_silu_kb_mask_kernel(tc, qT, kT, t, v, kb, mask, out):
         v_bf = tile("v_bf", [P, KV, E, PACK], BF16)
         v_codes = tile("v_codes", [P, KV * E], U32)
         v_scales = tile("v_scales", [P, KV * E], U8)
-        m_raw, mt, q_raw, q_bf, q_codes, q_scales = {}, {}, {}, {}, {}, {}
+        raw, mt, q_bf, q_codes, q_scales = {}, {}, {}, {}, {}
         p_sb, w_bf, w_codes, w_scales, y_sb = {}, {}, {}, {}, {}
-        for i, W in enumerate(RANGES):
-            m_raw[i] = tile("m_raw%d" % i, [P, PACK, W], F32)
-            mt[i] = tile("mt%d" % i, [P, PACK, W], F32)
-            for s in ["AB"] if JOINT[i] else "AB":
-                for g in range(2):
-                    both = tile("p_sb%s%d%d" % (s, i, g), [P, PACK, len(s), W], F32)
-                    p_sb[s, i, g] = both[:].rearrange("p r s n -> p r (s n)")
-                    for x, c in enumerate(s):
-                        p_sb[c + str(i) + str(g)] = both[:, :, x, :]
-            for s in "AB":
+        for name, (a, W) in LOADS.items():
+            raw[name] = tile("raw" + name, [P, PACK, W], F32)
+            if name[0] == "m":
+                mt[name] = tile("mt" + name, [P, PACK, W], F32)
+        for s in "MO":
+            for i, (a, W) in enumerate(PIECES[s]):
                 u = s + str(i)
-                q_raw[u] = tile("q_raw" + u, [P, PACK, W], F32)
                 q_bf[u] = tile("q_bf" + u, [P, W, PACK], BF16)
                 q_codes[u] = tile("q_codes" + u, [P, W], U32)
                 q_scales[u] = tile("q_scales" + u, [P, W], U8)
-                for g in range(2):
-                    n = u + str(g)
+            for g in range(2):
+                for i, (a, W) in enumerate(UNITS[s]):
+                    p_sb[s, i, g] = tile("p_sb%s%d%d" % (s, i, g), [P, PACK, W], F32)
+                for i, (a, W) in enumerate(CHUNKS[s]):
+                    n = "%s%d%d" % (s, i, g)
                     w_bf[n] = tile("w_bf" + n, [P, W, PACK], BF16)
                     w_codes[n] = tile("w_codes" + n, [P, W], U32)
                     w_scales[n] = tile("w_scales" + n, [P, W], U8)
                     y_sb[n] = tile("y_sb" + n, [P, W], F32)
+
+        def holder(spans, col):
+            return [i for i, (a, W) in enumerate(spans) if a <= col < a + W][0]
+
+        def load_of(kind, col):
+            return [name for name, (a, W) in LOADS.items() if name[0] == kind and a <= col < a + W][0]
 
         def copy(eng, dst, src):
             if eng == "V":
@@ -94,13 +102,11 @@ def tile_rows_a_silu_kb_mask_kernel(tc, qT, kT, t, v, kb, mask, out):
         def quantize(codes, scales, src):
             nc.vector.quantize_mx(out=codes[:].bitcast(FP8X4), scales=scales[:], in_=src)
 
-        def load_q(queue, u, g):
-            i = int(u[1])
-            h = 2 * g + "AB".index(u[0])
-            cols = slice(starts[i], starts[i] + RANGES[i])
+        def load_half(queue, name, g):
+            a, W = LOADS[name]
             queue.dma_start(
-                out=q_raw[u][ROWS * g : ROWS * (g + 1), :, :],
-                in_=qT[h].rearrange("(p j) n -> p j n", j=PACK)[:, :, cols],
+                out=raw[name][ROWS * g : ROWS * (g + 1), :, :],
+                in_=qT[HEADS["O"][g]].rearrange("(p j) n -> p j n", j=PACK)[:, :, a : a + W],
             )
 
         def load(name):
@@ -111,12 +117,14 @@ def tile_rows_a_silu_kb_mask_kernel(tc, qT, kT, t, v, kb, mask, out):
                     out=v_raw[:].rearrange("p g j e -> p g (j e)"),
                     in_=v.rearrange("g (p j) e -> p g (j e)", j=PACK),
                 )
-            elif name[0] == "m":
-                i = int(name[1])
-                cols = slice(starts[i], starts[i] + RANGES[i])
-                nc.sync.dma_start(out=m_raw[i][:], in_=mask.rearrange("(p j) n -> p j n", j=PACK)[:, :, cols])
+            elif name[0] == "O":
+                load_half(nc.sync, name, 0)
+                if not RING:
+                    load_half(nc.sync, name, 1)
             else:
-                load_q(nc.sync, name[1:], 0)
+                a, W = LOADS[name]
+                src = mask if name[0] == "m" else qT[1:3].rearrange("g d n -> (g d) n")
+                nc.sync.dma_start(out=raw[name][:], in_=src.rearrange("(p j) n -> p j n", j=PACK)[:, :, a : a + W])
 
         nc.scalar.dma_start(out=kb_sb[:], in_=kb.rearrange("(p j) o -> p (j o)", j=PACK))
         nc.scalar.dma_start(out=t_sb[:], in_=t.rearrange("(p j) o -> p (j o)", j=PACK))
@@ -129,7 +137,7 @@ def tile_rows_a_silu_kb_mask_kernel(tc, qT, kT, t, v, kb, mask, out):
             if kind == "L":
                 load(name[1:])
             elif kind == "d":
-                load_q(nc.scalar, name[1:], 1)
+                load_half(nc.scalar, name[1:], 1)
             elif name[:2] == "ck":
                 x = int(name[2])
                 copy(
@@ -150,70 +158,78 @@ def tile_rows_a_silu_kb_mask_kernel(tc, qT, kT, t, v, kb, mask, out):
             elif name == "Qv":
                 quantize(v_codes, v_scales, v_bf[:].rearrange("p g e j -> p (g e j)"))
             elif name[:2] == "mt":
-                i = int(name[2])
+                i = "m" + name[2]
                 for r in (2 * int(name[3]), 2 * int(name[3]) + 1):
                     if eng == "V":
                         nc.vector.tensor_scalar(
-                            out=mt[i][:, r, :], in0=m_raw[i][:, r, :], scalar1=t_sb[:, r : r + 1], scalar2=None, op0=ALU.mult
+                            out=mt[i][:, r, :], in0=raw[i][:, r, :], scalar1=t_sb[:, r : r + 1], scalar2=None, op0=ALU.mult
                         )
                     else:
-                        nc.scalar.activation(out=mt[i][:, r, :], in_=m_raw[i][:, r, :], func=ACT.Copy, scale=t_sb[:, r : r + 1])
+                        nc.scalar.activation(out=mt[i][:, r, :], in_=raw[i][:, r, :], func=ACT.Copy, scale=t_sb[:, r : r + 1])
             elif name[:2] == "cq":
                 u = name[2:]
+                a, W = PIECES[u[0]][int(u[1])]
+                src = load_of(u[0], a)
+                a -= LOADS[src][0]
                 copy(
                     eng,
                     q_bf[u][:].rearrange("p (c i) j -> p c j i", i=RUN),
-                    q_raw[u][:].rearrange("p j (c i) -> p c j i", i=RUN),
+                    raw[src][:, :, a : a + W].rearrange("p j (c i) -> p c j i", i=RUN),
                 )
             elif name[:2] == "Qq":
                 u = name[2:]
                 quantize(q_codes[u], q_scales[u], q_bf[u][:].rearrange("p n j -> p (n j)"))
             elif kind == "s":
-                i, b = int(name[2]), int(name[3])
-                sets = "AB" if name[1] == "J" else name[1]
-                W = RANGES[i]
-                per = 2 if W * len(sets) <= 256 else 1
+                s, i, b = name[1], int(name[2]), int(name[3])
+                a, W = UNITS[s][i]
+                per = 2 if W <= PER else 1
                 slot = used["s"] % 3
                 used["s"] += 1
                 where[name] = slot
                 col = 0
                 for r in range(per * b, per * (b + 1)):
                     kc = slice((r % 2) * P, (r % 2 + 1) * P)
-                    for s in sets:
-                        u = s + str(i)
-                        for c in range(0, W, P):
-                            for g in range(2):
-                                rows = slice(ROWS * g, ROWS * (g + 1))
-                                nc.tensor.matmul_mx(
-                                    out=score_banks[g][slot][:, col : col + P],
-                                    lhsT=k_codes[r // 2][rows, kc].bitcast(FP8X4),
-                                    lhsT_scale=k_scales[r // 2][rows, kc],
-                                    rhs=q_codes[u][rows, c : c + P].bitcast(FP8X4),
-                                    rhs_scale=q_scales[u][rows, c : c + P],
-                                    start=True,
-                                    stop=True,
-                                )
-                            col += P
+                    for c in range(a, a + W, P):
+                        x = holder(PIECES[s], c)
+                        u = s + str(x)
+                        qc = slice(c - PIECES[s][x][0], c - PIECES[s][x][0] + P)
+                        for g in range(2):
+                            rows = slice(ROWS * g, ROWS * (g + 1))
+                            nc.tensor.matmul_mx(
+                                out=score_banks[g][slot][:, col : col + P],
+                                lhsT=k_codes[r // 2][rows, kc].bitcast(FP8X4),
+                                lhsT_scale=k_scales[r // 2][rows, kc],
+                                rhs=q_codes[u][rows, qc].bitcast(FP8X4),
+                                rhs_scale=q_scales[u][rows, qc],
+                                start=True,
+                                stop=True,
+                            )
+                        col += P
             elif kind == "a":
-                i, g, b = int(name[2]), int(name[3]), int(name[4])
-                sets = "AB" if name[1] == "J" else name[1]
-                AW = RANGES[i] * len(sets)
-                per = 2 if AW <= 256 else 1
+                s, i, g, b = name[1], int(name[2]), int(name[3]), int(name[4])
+                a, W = UNITS[s][i]
+                per = 2 if W <= PER else 1
                 bank = score_banks[g][where["s" + name[1:3] + name[4]]]
                 for x in range(per):
                     r = per * b + x
                     nc.scalar.activation(
-                        out=p_sb[sets, i, g][:, r, :],
-                        in_=bank[:, x * AW : (x + 1) * AW],
+                        out=p_sb[s, i, g][:, r, :],
+                        in_=bank[:, x * W : (x + 1) * W],
                         func=ACT.Silu,
                         bias=kb_sb[:, r : r + 1],
                     )
             elif kind == "T":
                 n = name[1:]
+                s, g = n[0], int(n[2])
+                a, W = CHUNKS[s][int(n[1])]
+                i = holder(UNITS[s], a)
+                pa = a - UNITS[s][i][0]
+                m = load_of("m", a)
+                ma = a - LOADS[m][0]
                 nc.vector.tensor_tensor(
                     out=w_bf[n][:].rearrange("p (c i) r -> p c r i", i=RUN),
-                    in0=p_sb[n].rearrange("p r (c i) -> p c r i", i=RUN),
-                    in1=mt[int(n[1])][:].rearrange("p r (c i) -> p c r i", i=RUN),
+                    in0=p_sb[s, i, g][:, :, pa : pa + W].rearrange("p r (c i) -> p c r i", i=RUN),
+                    in1=mt[m][:, :, ma : ma + W].rearrange("p r (c i) -> p c r i", i=RUN),
                     op=ALU.mult,
                 )
             elif kind == "W":
@@ -222,7 +238,7 @@ def tile_rows_a_silu_kb_mask_kernel(tc, qT, kT, t, v, kb, mask, out):
             elif kind == "p":
                 n = name[1:]
                 g = int(n[2])
-                W = RANGES[int(n[1])]
+                W = CHUNKS[n[0]][int(n[1])][1]
                 bank = y_banks[used["y"] % 2]
                 used["y"] += 1
                 where[n] = bank[:, 0:W]
@@ -238,13 +254,13 @@ def tile_rows_a_silu_kb_mask_kernel(tc, qT, kT, t, v, kb, mask, out):
                     )
             else:
                 n = name[1:]
-                i, g = int(n[1]), int(n[2])
-                h = 2 * g + "AB".index(n[0])
+                a, W = CHUNKS[n[0]][int(n[1])]
+                h = HEADS[n[0]][int(n[2])]
                 if eng == "V":
                     nc.vector.tensor_scalar(out=y_sb[n][:], in0=where[n], scalar1=1.0 / 16.0, scalar2=None, op0=ALU.mult)
                 else:
                     nc.scalar.activation(out=y_sb[n][:], in_=where[n], func=ACT.Copy, scale=1.0 / 16.0)
                 nc.sync.dma_start(
-                    out=out[h, starts[i] : starts[i] + RANGES[i], :].rearrange("(c p) e -> p c e", p=P),
+                    out=out[h, a : a + W, :].rearrange("(c p) e -> p c e", p=P),
                     in_=y_sb[n][:].rearrange("p (c e) -> p c e", e=E),
                 )

@@ -2,25 +2,25 @@ from contextlib import ExitStack
 
 import concourse.mybir as mybir
 
-LOADS = {'M0': (0, 128), 'm0': (0, 128), 'O0': (0, 128), 'M1': (128, 256), 'm1': (128, 256), 'O1': (128, 256), 'M2': (384, 128), 'm2': (384, 128), 'O2': (384, 128)}
-PIECES = {'M': [(0, 128), (128, 256), (384, 128)], 'O': [(0, 128), (128, 256), (384, 128)]}
-UNITS = {'M': [(0, 128), (128, 256), (384, 128)], 'O': [(0, 128), (128, 256), (384, 128)]}
-CHUNKS = {'M': [(0, 128), (128, 256), (384, 128)], 'O': [(0, 128), (128, 256), (384, 128)]}
+LOADS = {'M0': (0, 256), 'm0': (0, 256), 'M1': (256, 256), 'O0': (0, 256), 'm1': (256, 256), 'O1': (256, 256)}
+PIECES = {'M': [(0, 128), (128, 128), (256, 256)], 'O': [(0, 256), (256, 256)]}
+UNITS = {'M': [(0, 128, 1), (128, 128, 2), (256, 256, 1)], 'O': [(0, 256, 1), (256, 256, 1)], 'J': []}
+CHUNKS = {'M': [(0, 128), (128, 128), (256, 256)], 'O': [(0, 256), (256, 128), (384, 128)]}
 RUN = 2
 PER = 128
 RING = 0
 ORDER = """
-Lk:Y LM0:Y Lm0:Y LO0:Y LM1:Y Lm1:Y LO1:Y LM2:Y Lm2:Y Lv:Y LO2:Y ck0:V
-ck1:S cqM0:V Qk0:V QqM0:V Qk1:V mt01:S sM00:P mt00:V sM01:P aM000:S cqO0:V aM001:S
-QqO0:V aM011:S TM00:V aM010:S sO00:P cqM1:V sO01:P aO010:S WM00:V aO000:S QqM1:V aO011:S
-TM01:V aO001:S sM11:P TO01:V mt10:S sM12:P WM01:V aM111:S TO00:V sM13:P aM101:S mt11:V
-aM102:S sM10:P aM113:S WO00:V WO01:V aM103:S cqO1:V aM112:S aM110:S cqM2:S QqO1:V TM11:V
-aM100:S sO12:P mt20:S sO10:P mt21:S TM10:V aO112:S sO13:P aO102:S cv1:S sO11:P cv0:V
-WM10:V aO100:S Qv:V aO110:S QqM2:V aO111:S cqO2:V pO01:P aO113:S pM01:P WM11:V sM20:P
-aO103:S QqO2:V eO01:S TO11:V eM01:S pM00:P aO101:S pO00:P sO20:P aM200:S eM00:S TO10:V
-sM21:P aM210:S aO200:S pM10:P sO21:P eO00:S aM211:S WO11:V WO10:V pM11:P aM201:S TM21:V
-eM10:S eM11:S pO10:P TM20:V aO201:S pO11:P aO210:S WM21:V TO20:V aO211:S eO10:S WM20:V
-TO21:V eO11:S pM20:P pM21:P WO20:V eM20:S WO21:V eM21:S pO20:P pO21:P eO20:S eO21:V
+Lk:Y LM0:Y LM1:Y Lm0:Y LO0:Y Lm1:Y LO1:Y Lv:Y ck0:V ck1:S Qk0:V cqM0:V
+cqM1:S QqM0:V Qk1:V sM00:P QqM1:V sM01:P aM000:S sM02:P cqM2:V aM010:S aM001:S sM03:P
+aM011:S aM002:S sM10:P QqM2:V aM003:S aM012:S aM013:S mt00:V sM11:P aM100:S mt01:V aM110:S
+sM20:P TM00:V aM101:S sM21:P aM111:S TM01:V aM200:S sM22:P aM210:S TM10:V aM201:S sM23:P
+cqO0:V aM211:S aM202:S WM00:V aM203:S QqO0:V aM212:S WM01:V mt11:S WM10:V sO00:P mt10:V
+TM11:V aM213:S sO01:P aO000:S TM20:V sO02:P aO010:S aO001:S sO03:P aO011:S TM21:V aO002:S
+cqO1:S WM20:V cv0:V aO003:S QqO1:V aO012:S WM11:V aO013:S TO00:V sO10:P cv1:S sO11:P
+aO100:S Qv:V sO12:P aO110:S WO00:V aO101:S TO01:V pM00:P aO111:S pM01:P sO13:P eM00:S
+eM01:S aO102:S pM10:P pM11:P WM21:V aO103:S WO01:V eM10:S eM11:S TO10:V pM20:P aO112:S
+pM21:P aO113:S TO20:V eM20:S eM21:S WO10:V pO00:P TO11:V pO01:P eO00:S WO20:V TO21:V
+eO01:S pO10:P pO20:P WO11:V eO10:S WO21:V eO20:S pO11:P pO21:P eO11:S eO21:V
 """
 
 F32 = mybir.dt.float32
@@ -78,7 +78,7 @@ def tile_rows_a_silu_kb_mask_kernel(tc, qT, kT, t, v, kb, mask, out):
                 q_codes[u] = tile("q_codes" + u, [P, W], U32)
                 q_scales[u] = tile("q_scales" + u, [P, W], U8)
             for g in range(2):
-                for i, (a, W) in enumerate(UNITS[s]):
+                for i, (a, W, per) in enumerate(UNITS[s]):
                     p_sb[s, i, g] = tile("p_sb%s%d%d" % (s, i, g), [P, PACK, W], F32)
                 for i, (a, W) in enumerate(CHUNKS[s]):
                     n = "%s%d%d" % (s, i, g)
@@ -88,7 +88,7 @@ def tile_rows_a_silu_kb_mask_kernel(tc, qT, kT, t, v, kb, mask, out):
                     y_sb[n] = tile("y_sb" + n, [P, W], F32)
 
         def holder(spans, col):
-            return [i for i, (a, W) in enumerate(spans) if a <= col < a + W][0]
+            return [i for i, span in enumerate(spans) if span[0] <= col < span[0] + span[1]][0]
 
         def load_of(kind, col):
             return [name for name, (a, W) in LOADS.items() if name[0] == kind and a <= col < a + W][0]
@@ -125,9 +125,10 @@ def tile_rows_a_silu_kb_mask_kernel(tc, qT, kT, t, v, kb, mask, out):
                 a, W = LOADS[name]
                 src = mask if name[0] == "m" else qT[1:3].rearrange("g d n -> (g d) n")
                 nc.sync.dma_start(out=raw[name][:], in_=src.rearrange("(p j) n -> p j n", j=PACK)[:, :, a : a + W])
+                if name == "M0":
+                    nc.sync.dma_start(out=kb_sb[:], in_=kb.rearrange("(p j) o -> p (j o)", j=PACK))
+                    nc.sync.dma_start(out=t_sb[:], in_=t.rearrange("(p j) o -> p (j o)", j=PACK))
 
-        nc.scalar.dma_start(out=kb_sb[:], in_=kb.rearrange("(p j) o -> p (j o)", j=PACK))
-        nc.scalar.dma_start(out=t_sb[:], in_=t.rearrange("(p j) o -> p (j o)", j=PACK))
         nc.vector.memset(warm[:, 0:1], 0.0)
         nc.scalar.activation(out=warm[:, 1:2], in_=warm[:, 0:1], func=ACT.Silu)
 
@@ -181,8 +182,7 @@ def tile_rows_a_silu_kb_mask_kernel(tc, qT, kT, t, v, kb, mask, out):
                 quantize(q_codes[u], q_scales[u], q_bf[u][:].rearrange("p n j -> p (n j)"))
             elif kind == "s":
                 s, i, b = name[1], int(name[2]), int(name[3])
-                a, W = UNITS[s][i]
-                per = 2 if W <= PER else 1
+                a, W, per = UNITS[s][i]
                 slot = used["s"] % 3
                 used["s"] += 1
                 where[name] = slot
@@ -207,8 +207,7 @@ def tile_rows_a_silu_kb_mask_kernel(tc, qT, kT, t, v, kb, mask, out):
                         col += P
             elif kind == "a":
                 s, i, g, b = name[1], int(name[2]), int(name[3]), int(name[4])
-                a, W = UNITS[s][i]
-                per = 2 if W <= PER else 1
+                a, W, per = UNITS[s][i]
                 bank = score_banks[g][where["s" + name[1:3] + name[4]]]
                 for x in range(per):
                     r = per * b + x

from contextlib import ExitStack

import concourse.mybir as mybir

LOADS = {'M0': (0, 256), 'm0': (0, 256), 'M1': (256, 256), 'O0': (0, 256), 'm1': (256, 256), 'O1': (256, 256)}
PIECES = {'M': [(0, 128), (128, 128), (256, 256)], 'O': [(0, 256), (256, 256)]}
UNITS = {'M': [(0, 128, 1), (128, 128, 2), (256, 256, 1)], 'O': [(0, 256, 1), (256, 256, 1)], 'J': []}
CHUNKS = {'M': [(0, 128), (128, 128), (256, 256)], 'O': [(0, 256), (256, 128), (384, 128)]}
RUN = 2
PER = 128
RING = 0
ORDER = """
Lk:Y LM0:Y LM1:Y Lm0:Y LO0:Y Lm1:Y LO1:Y Lv:Y ck0:V ck1:S Qk0:V cqM0:V
cqM1:S QqM0:V Qk1:V sM00:P QqM1:V sM01:P aM000:S sM02:P cqM2:V aM010:S aM001:S sM03:P
aM011:S aM002:S sM10:P QqM2:V aM003:S aM012:S aM013:S mt00:V sM11:P aM100:S mt01:V aM110:S
sM20:P TM00:V aM101:S sM21:P aM111:S TM01:V aM200:S sM22:P aM210:S TM10:V aM201:S sM23:P
cqO0:V aM211:S aM202:S WM00:V aM203:S QqO0:V aM212:S WM01:V mt11:S WM10:V sO00:P mt10:V
TM11:V aM213:S sO01:P aO000:S TM20:V sO02:P aO010:S aO001:S sO03:P aO011:S TM21:V aO002:S
cqO1:S WM20:V cv0:V aO003:S QqO1:V aO012:S WM11:V aO013:S TO00:V sO10:P cv1:S sO11:P
aO100:S Qv:V sO12:P aO110:S WO00:V aO101:S TO01:V pM00:P aO111:S pM01:P sO13:P eM00:S
eM01:S aO102:S pM10:P pM11:P WM21:V aO103:S WO01:V eM10:S eM11:S TO10:V pM20:P aO112:S
pM21:P aO113:S TO20:V eM20:S eM21:S WO10:V pO00:P TO11:V pO01:P eO00:S WO20:V TO21:V
eO01:S pO10:P pO20:P WO11:V eO10:S WO21:V eO20:S pO11:P pO21:P eO11:S eO21:V
"""

F32 = mybir.dt.float32
BF16 = mybir.dt.bfloat16
U32 = mybir.dt.uint32
U8 = mybir.dt.uint8
FP8X4 = mybir.dt.float8_e4m3fn_x4
ACT = mybir.ActivationFunctionType
ALU = mybir.AluOpType

H, KV, D, NQ, N, E = 4, 2, 256, 512, 512, 128
P = 128
ROWS = 64
PACK = 4
HEADS = {"M": (1, 2), "O": (0, 3)}
FLOPS = 2 * H * NQ * N * (D + E)


def tile_rows_a_silu_kb_mask_kernel(tc, qT, kT, t, v, kb, mask, out):
    nc = tc.nc
    with ExitStack() as ctx:
        sb = ctx.enter_context(tc.tile_pool(name="sb", bufs=1))
        ps = ctx.enter_context(tc.psum_pool(name="ps", bufs=1))
        ctx.enter_context(tc.manual_schedule())

        def tile(name, shape, dtype):
            return sb.tile(shape, dtype, name=name, align_bytes=64)

        score_banks = [[ps.tile([P, 512], F32, name="score%d%d" % (g, b)) for b in range(3)] for g in range(2)]
        y_banks = [ps.tile([P, 512], F32, name="ybank%d" % b) for b in range(2)]
        used = {"s": 0, "y": 0}
        where = {}

        t_sb = tile("t_sb", [P, PACK], F32)
        kb_sb = tile("kb_sb", [P, PACK], F32)
        warm = tile("warm", [P, 2], F32)
        k_raw = tile("k_raw", [P, PACK, N], F32)
        k_bf = [tile("k_bf%d" % x, [P, 2, P, PACK], BF16) for x in range(2)]
        k_codes = [tile("k_codes%d" % x, [P, 2 * P], U32) for x in range(2)]
        k_scales = [tile("k_scales%d" % x, [P, 2 * P], U8) for x in range(2)]
        v_raw = tile("v_raw", [P, KV, PACK, E], F32)
        v_bf = tile("v_bf", [P, KV, E, PACK], BF16)
        v_codes = tile("v_codes", [P, KV * E], U32)
        v_scales = tile("v_scales", [P, KV * E], U8)
        raw, mt, q_bf, q_codes, q_scales = {}, {}, {}, {}, {}
        p_sb, w_bf, w_codes, w_scales, y_sb = {}, {}, {}, {}, {}
        for name, (a, W) in LOADS.items():
            raw[name] = tile("raw" + name, [P, PACK, W], F32)
            if name[0] == "m":
                mt[name] = tile("mt" + name, [P, PACK, W], F32)
        for s in "MO":
            for i, (a, W) in enumerate(PIECES[s]):
                u = s + str(i)
                q_bf[u] = tile("q_bf" + u, [P, W, PACK], BF16)
                q_codes[u] = tile("q_codes" + u, [P, W], U32)
                q_scales[u] = tile("q_scales" + u, [P, W], U8)
            for g in range(2):
                for i, (a, W, per) in enumerate(UNITS[s]):
                    p_sb[s, i, g] = tile("p_sb%s%d%d" % (s, i, g), [P, PACK, W], F32)
                for i, (a, W) in enumerate(CHUNKS[s]):
                    n = "%s%d%d" % (s, i, g)
                    w_bf[n] = tile("w_bf" + n, [P, W, PACK], BF16)
                    w_codes[n] = tile("w_codes" + n, [P, W], U32)
                    w_scales[n] = tile("w_scales" + n, [P, W], U8)
                    y_sb[n] = tile("y_sb" + n, [P, W], F32)

        def holder(spans, col):
            return [i for i, span in enumerate(spans) if span[0] <= col < span[0] + span[1]][0]

        def load_of(kind, col):
            return [name for name, (a, W) in LOADS.items() if name[0] == kind and a <= col < a + W][0]

        def copy(eng, dst, src):
            if eng == "V":
                nc.vector.tensor_copy(out=dst, in_=src)
            else:
                nc.scalar.copy(out=dst, in_=src)

        def quantize(codes, scales, src):
            nc.vector.quantize_mx(out=codes[:].bitcast(FP8X4), scales=scales[:], in_=src)

        def load_half(queue, name, g):
            a, W = LOADS[name]
            queue.dma_start(
                out=raw[name][ROWS * g : ROWS * (g + 1), :, :],
                in_=qT[HEADS["O"][g]].rearrange("(p j) n -> p j n", j=PACK)[:, :, a : a + W],
            )

        def load(name):
            if name == "k":
                nc.sync.dma_start(out=k_raw[:], in_=kT.rearrange("g (p j) n -> (g p) j n", j=PACK))
            elif name == "v":
                nc.sync.dma_start(
                    out=v_raw[:].rearrange("p g j e -> p g (j e)"),
                    in_=v.rearrange("g (p j) e -> p g (j e)", j=PACK),
                )
            elif name[0] == "O":
                load_half(nc.sync, name, 0)
                if not RING:
                    load_half(nc.sync, name, 1)
            else:
                a, W = LOADS[name]
                src = mask if name[0] == "m" else qT[1:3].rearrange("g d n -> (g d) n")
                nc.sync.dma_start(out=raw[name][:], in_=src.rearrange("(p j) n -> p j n", j=PACK)[:, :, a : a + W])
                if name == "M0":
                    nc.sync.dma_start(out=kb_sb[:], in_=kb.rearrange("(p j) o -> p (j o)", j=PACK))
                    nc.sync.dma_start(out=t_sb[:], in_=t.rearrange("(p j) o -> p (j o)", j=PACK))

        nc.vector.memset(warm[:, 0:1], 0.0)
        nc.scalar.activation(out=warm[:, 1:2], in_=warm[:, 0:1], func=ACT.Silu)

        for step in ORDER.split():
            name, eng = step.split(":")
            kind = name[0]
            if kind == "L":
                load(name[1:])
            elif kind == "d":
                load_half(nc.scalar, name[1:], 1)
            elif name[:2] == "ck":
                x = int(name[2])
                copy(
                    eng,
                    k_bf[x][:].rearrange("p r s j -> p s j r"),
                    k_raw[:].rearrange("p j (s r) -> p s j r", r=PACK)[:, :, :, 2 * x : 2 * x + 2],
                )
            elif name[:2] == "Qk":
                x = int(name[2])
                quantize(k_codes[x], k_scales[x], k_bf[x][:].rearrange("p r s j -> p (r s j)"))
            elif name[:2] == "cv":
                g = int(name[2])
                copy(
                    eng,
                    v_bf[:, g].rearrange("p (c i) j -> p c j i", i=RUN),
                    v_raw[:, g].rearrange("p j (c i) -> p c j i", i=RUN),
                )
            elif name == "Qv":
                quantize(v_codes, v_scales, v_bf[:].rearrange("p g e j -> p (g e j)"))
            elif name[:2] == "mt":
                i = "m" + name[2]
                for r in (2 * int(name[3]), 2 * int(name[3]) + 1):
                    if eng == "V":
                        nc.vector.tensor_scalar(
                            out=mt[i][:, r, :], in0=raw[i][:, r, :], scalar1=t_sb[:, r : r + 1], scalar2=None, op0=ALU.mult
                        )
                    else:
                        nc.scalar.activation(out=mt[i][:, r, :], in_=raw[i][:, r, :], func=ACT.Copy, scale=t_sb[:, r : r + 1])
            elif name[:2] == "cq":
                u = name[2:]
                a, W = PIECES[u[0]][int(u[1])]
                src = load_of(u[0], a)
                a -= LOADS[src][0]
                copy(
                    eng,
                    q_bf[u][:].rearrange("p (c i) j -> p c j i", i=RUN),
                    raw[src][:, :, a : a + W].rearrange("p j (c i) -> p c j i", i=RUN),
                )
            elif name[:2] == "Qq":
                u = name[2:]
                quantize(q_codes[u], q_scales[u], q_bf[u][:].rearrange("p n j -> p (n j)"))
            elif kind == "s":
                s, i, b = name[1], int(name[2]), int(name[3])
                a, W, per = UNITS[s][i]
                slot = used["s"] % 3
                used["s"] += 1
                where[name] = slot
                col = 0
                for r in range(per * b, per * (b + 1)):
                    kc = slice((r % 2) * P, (r % 2 + 1) * P)
                    for c in range(a, a + W, P):
                        x = holder(PIECES[s], c)
                        u = s + str(x)
                        qc = slice(c - PIECES[s][x][0], c - PIECES[s][x][0] + P)
                        for g in range(2):
                            rows = slice(ROWS * g, ROWS * (g + 1))
                            nc.tensor.matmul_mx(
                                out=score_banks[g][slot][:, col : col + P],
                                lhsT=k_codes[r // 2][rows, kc].bitcast(FP8X4),
                                lhsT_scale=k_scales[r // 2][rows, kc],
                                rhs=q_codes[u][rows, qc].bitcast(FP8X4),
                                rhs_scale=q_scales[u][rows, qc],
                                start=True,
                                stop=True,
                            )
                        col += P
            elif kind == "a":
                s, i, g, b = name[1], int(name[2]), int(name[3]), int(name[4])
                a, W, per = UNITS[s][i]
                bank = score_banks[g][where["s" + name[1:3] + name[4]]]
                for x in range(per):
                    r = per * b + x
                    nc.scalar.activation(
                        out=p_sb[s, i, g][:, r, :],
                        in_=bank[:, x * W : (x + 1) * W],
                        func=ACT.Silu,
                        bias=kb_sb[:, r : r + 1],
                    )
            elif kind == "T":
                n = name[1:]
                s, g = n[0], int(n[2])
                a, W = CHUNKS[s][int(n[1])]
                i = holder(UNITS[s], a)
                pa = a - UNITS[s][i][0]
                m = load_of("m", a)
                ma = a - LOADS[m][0]
                nc.vector.tensor_tensor(
                    out=w_bf[n][:].rearrange("p (c i) r -> p c r i", i=RUN),
                    in0=p_sb[s, i, g][:, :, pa : pa + W].rearrange("p r (c i) -> p c r i", i=RUN),
                    in1=mt[m][:, :, ma : ma + W].rearrange("p r (c i) -> p c r i", i=RUN),
                    op=ALU.mult,
                )
            elif kind == "W":
                n = name[1:]
                quantize(w_codes[n], w_scales[n], w_bf[n][:].rearrange("p n r -> p (n r)"))
            elif kind == "p":
                n = name[1:]
                g = int(n[2])
                W = CHUNKS[n[0]][int(n[1])][1]
                bank = y_banks[used["y"] % 2]
                used["y"] += 1
                where[n] = bank[:, 0:W]
                for c in range(0, W, P):
                    nc.tensor.matmul_mx(
                        out=bank[:, c : c + P],
                        lhsT=w_codes[n][:, c : c + P].bitcast(FP8X4),
                        lhsT_scale=w_scales[n][:, c : c + P],
                        rhs=v_codes[:, g * E : (g + 1) * E].bitcast(FP8X4),
                        rhs_scale=v_scales[:, g * E : (g + 1) * E],
                        start=True,
                        stop=True,
                    )
            else:
                n = name[1:]
                a, W = CHUNKS[n[0]][int(n[1])]
                h = HEADS[n[0]][int(n[2])]
                if eng == "V":
                    nc.vector.tensor_scalar(out=y_sb[n][:], in0=where[n], scalar1=1.0 / 16.0, scalar2=None, op0=ALU.mult)
                else:
                    nc.scalar.activation(out=y_sb[n][:], in_=where[n], func=ACT.Copy, scale=1.0 / 16.0)
                nc.sync.dma_start(
                    out=out[h, a : a + W, :].rearrange("(c p) e -> p c e", p=P),
                    in_=y_sb[n][:].rearrange("p (c e) -> p c e", e=E),
                )
